import numpy as np
import ml_dtypes


def mxq(x, axis, fmt="e4m3"):
    dtype, down = {"e4m3": (ml_dtypes.float8_e4m3fn, 7), "e5m2": (ml_dtypes.float8_e5m2, 14)}[fmt]
    v = np.moveaxis(np.asarray(x, np.float32).astype(ml_dtypes.bfloat16).astype(np.float64), axis, -1)
    blocks = v.reshape(v.shape[:-1] + (-1, 32))
    amax = np.abs(blocks).max(-1, keepdims=True)
    byte = np.maximum(np.where(amax > 0, np.frexp(amax)[1] - 1 + 127, 0) - down, 1)
    scale = np.exp2(byte - 127.0)
    codes = (blocks / scale).astype(np.float32).astype(dtype).astype(np.float64)
    return np.moveaxis((codes * scale).reshape(v.shape), -1, axis)


WIDE = False


def mx_kscale(k):
    if not WIDE:
        return np.ones(k)
    levels = np.array([30, -30])
    if k % 512:
        return np.exp2(np.random.permutation(np.resize(levels, k // 32))).repeat(32)
    a = np.empty((k // 512, 16))
    for p in range(k // 512):
        a[p, :8] = np.random.permutation(np.resize(levels, 8))
        for g in range(8):
            far = levels[np.abs(levels - a[p, g]) >= 10]
            a[p, g + 8] = far[np.random.randint(len(far))]
    return np.exp2(a.ravel()).repeat(32)


def f64(x):
    return np.asarray(x).astype(np.float64)


def striped(idx):
    return np.tile(np.asarray(idx).reshape(-1, 16).T, (8, 1)).astype(np.uint16)


def unstriped(offs):
    return offs[:16].T.reshape(-1).astype(np.int64)


E2M1 = np.array([0.0, 0.5, 1.0, 1.5, 2.0, 3.0, 4.0, 6.0, -0.0, -0.5, -1.0, -1.5, -2.0, -3.0, -4.0, -6.0])


def pack_weight(w, fmt):
    k, n = w.shape
    w = f64(np.asarray(w, np.float32).astype(ml_dtypes.bfloat16)).reshape(k // 32, 32, n)
    amax = np.abs(w).max(1)
    if fmt in ("e4m3", "e5m2"):
        byte = np.frexp(amax)[1] - 1 + 127 - (7 if fmt == "e4m3" else 14)
    else:
        mant, ex = np.frexp(amax / 6.0)
        byte = np.where(mant > 0.5, ex, ex - 1) + 127
    byte = np.clip(np.where(amax > 0, byte, 1), 1, 254)
    scaled = (w * np.exp2(127.0 - byte)[:, None, :]).reshape(k, n).astype(np.float32)
    by_word = np.ascontiguousarray(scaled.reshape(k // 512, 128, 4, n).transpose(0, 1, 3, 2))
    if fmt in ("e4m3", "e5m2"):
        words = by_word.astype(ml_dtypes.float8_e4m3fn if fmt == "e4m3" else ml_dtypes.float8_e5m2).view(np.uint8)
    else:
        c = by_word.astype(ml_dtypes.float4_e2m1fn).view(np.uint8) & 0xF
        words = (c[..., 0::2] | (c[..., 1::2] << 4)).reshape(k // 512, 128, 2 * n)
    return np.ascontiguousarray(words), np.ascontiguousarray(byte.astype(np.uint8).reshape(k // 512, 16, n))


def unpack_weight(words, scales, fmt):
    g, _, n = scales.shape
    words = np.ascontiguousarray(words).reshape(g, 128, n, -1)
    if fmt in ("e4m3", "e5m2"):
        vals = words.view(ml_dtypes.float8_e4m3fn if fmt == "e4m3" else ml_dtypes.float8_e5m2).astype(np.float64)
    else:
        nib = np.empty((g, 128, n, 4), np.uint8)
        nib[..., 0::2] = words & 0xF
        nib[..., 1::2] = words >> 4
        vals = E2M1[nib]
    vals = vals * np.repeat(np.exp2(scales.astype(np.float64) - 127.0), 8, axis=1)[..., None]
    return vals.transpose(0, 1, 3, 2).reshape(g * 512, n)


K, T, Z, J, R, N, S = 512, 1024, 1024, 256, 512, 256, 1024


def setup_inputs():
    n = np.random.standard_normal
    idx = np.random.permutation(T)[:J]
    idx2 = np.random.permutation(Z)[:J]
    idx3 = np.random.permutation(J)[:J]
    idx4 = np.random.permutation(J)[:J]
    idx5 = np.random.permutation(S)[:N]
    fk = mx_kscale(K)
    fr = mx_kscale(R)
    xtp = pack_weight(n((K, T)) / fk[:, None], "e4m3")
    xop = pack_weight(n((K, Z)) / fk[:, None], "e2m1")
    wp = pack_weight(n((K, R)) * 1 / np.sqrt(K) * fk[:, None] * fr, "e5m2")
    vsp = pack_weight(n((R, S)) * 1 / np.sqrt(R) / fr[:, None], "e5m2")
    return {
        "xt_words": xtp[0],
        "xt_scales": xtp[1],
        "xo_words": xop[0],
        "xo_scales": xop[1],
        "w_words": wp[0],
        "w_scales": wp[1],
        "vs_words": vsp[0],
        "vs_scales": vsp[1],
        "offs": striped(idx),
        "offs2": striped(idx2),
        "offs3": striped(idx3),
        "offs4": striped(idx4),
        "offs5": striped(idx5),
    }


def reference(xt_words, xt_scales, xo_words, xo_scales, w_words, w_scales, vs_words, vs_scales, offs, offs2, offs3, offs4, offs5):
    idx = unstriped(offs)
    idx2 = unstriped(offs2)
    idx3 = unstriped(offs3)
    idx4 = unstriped(offs4)
    idx5 = unstriped(offs5)
    xtu = unpack_weight(xt_words, xt_scales, "e4m3")
    xou = unpack_weight(xo_words, xo_scales, "e2m1")
    wu = unpack_weight(w_words, w_scales, "e5m2")
    vsu = unpack_weight(vs_words, vs_scales, "e5m2")
    xtidxg = xtu[:, idx]
    a = wu.T @ xtidxg
    xoidx2g = xou[:, idx2]
    b = wu.T @ xoidx2g
    h1 = np.maximum(a, b[:, idx3])
    hid = np.abs(b - h1[:, idx4])
    vsidx5g = vsu[:, idx5]
    hidq = mxq(hid, 0, "e4m3")
    y = vsidx5g.T @ hidq
    return y

@@ -1,0 +1,149 @@
+from contextlib import ExitStack
+
+import concourse.mybir as mybir
+
+K, T, J, R, N = 512, 1024, 256, 512, 256
+FLOPS = 2 * (2 * K * R * J + R * N * J)
+
+F32 = mybir.dt.float32
+BF16 = mybir.dt.bfloat16
+I32 = mybir.dt.int32
+U32 = mybir.dt.uint32
+U16 = mybir.dt.uint16
+U8 = mybir.dt.uint8
+E4M3 = mybir.dt.float8_e4m3fn_x4
+E5M2 = mybir.dt.float8_e5m2_x4
+E2M1 = mybir.dt.float4_e2m1fn_x4
+ALU = mybir.AluOpType
+ACT = mybir.ActivationFunctionType
+P = 128
+PACK = 4
+B_WINDOW = 352
+
+
+def tile_list_tworounds_oneforboth_store_plain_kernel(tc, xt_words, xt_scales, xo_words, xo_scales, w_words, w_scales, vs_words, vs_scales,
+                        offs, offs2, offs3, offs4, offs5, out):
+    nc = tc.nc
+    with ExitStack() as ctx:
+        sb = ctx.enter_context(tc.tile_pool(name="sb", bufs=1))
+        ps = ctx.enter_context(tc.psum_pool(name="ps", bufs=1))
+
+        def sbuf(name, cols, dtype):
+            return sb.tile([P, cols], dtype, name=name, align_bytes=64)
+
+        def load_list(name, src):
+            lst = sb.tile([P, J // 16], U16, name=name)
+            nc.sync.dma_start(lst[:], src)
+            return lst
+
+        def load_words(queue, tile, src):
+            queue.dma_start(tile[:].bitcast(I32), src.bitcast(I32))
+
+        def load_scale_rows(queue, plane, src, q):
+            queue.dma_start(plane[32 * q : 32 * q + 4, :].bitcast(I32), src[0, 4 * q : 4 * q + 4, :].bitcast(I32))
+
+        xo_w = sbuf("xo_w", T, U16)
+        xo_s = sbuf("xo_s", T, U8)
+        w_w = sbuf("w_w", R, U32)
+        w_s = sbuf("w_s", R, U8)
+        xt_w = sbuf("xt_w", T, U32)
+        xt_s = sbuf("xt_s", T, U8)
+        vs_w = sbuf("vs_w", T, U32)
+        vs_s = sbuf("vs_s", T, U8)
+        b_sb = [sbuf("b_sb%d" % t, B_WINDOW, F32) for t in range(PACK)]
+        h_sb = [sbuf("h_sb%d" % t, 2 * J, F32) for t in range(PACK)]
+
+        nc.vector.memset(xo_s[:].bitcast(I32), 0)
+        nc.gpsimd.memset(w_s[:].bitcast(I32), 0)
+        nc.vector.memset(xt_s[:].bitcast(I32), 0)
+        nc.vector.memset(vs_s[:].bitcast(I32), 0)
+
+        l2 = load_list("l2", offs2)
+        load_words(nc.sync, xo_w, xo_words[0])
+        load_words(nc.sync, w_w, w_words[0].rearrange("p n t -> p (n t)"))
+        for q in range(4):
+            load_scale_rows(nc.scalar, xo_s, xo_scales, q)
+        load_scale_rows(nc.scalar, w_s, w_scales, 0)
+        load_scale_rows(nc.gpsimd, w_s, w_scales, 2)
+        load_scale_rows(nc.gpsimd, w_s, w_scales, 3)
+        load_scale_rows(nc.sync, w_s, w_scales, 1)
+        l1 = load_list("l1", offs)
+        load_words(nc.sync, xt_w, xt_words[0].rearrange("p n t -> p (n t)"))
+        for q in range(4):
+            load_scale_rows(nc.sync, xt_s, xt_scales, q)
+        l3 = load_list("l3", offs3)
+        l4 = load_list("l4", offs4)
+        l5 = load_list("l5", offs5)
+        load_words(nc.sync, vs_w, vs_words[0].rearrange("p n t -> p (n t)"))
+        for q in range(4):
+            load_scale_rows(nc.sync, vs_s, vs_scales, q)
+        for t in range(PACK):
+            nc.gpsimd.memset(b_sb[t][:, J:], 0.0)
+
+        xo_gw = sbuf("xo_gw", J, U16)
+        xo_gs = sbuf("xo_gs", J, U8)
+        nc.vector.tensor_copy(xo_gw[:], xo_w[:].indirect(l2[:]))
+        nc.vector.tensor_copy(xo_gs[:], xo_s[:].indirect(l2[:]))
+        w_pw = sbuf("w_pw", R, U32)
+        w_ps = sbuf("w_ps", R, U8)
+        nc.vector.tensor_copy(w_pw[:].rearrange("p (t m) -> p t m", t=PACK), w_w[:].rearrange("p (m t) -> p t m", t=PACK))
+        nc.vector.tensor_copy(w_ps[:].rearrange("p (t m) -> p t m", t=PACK), w_s[:].rearrange("p (m t) -> p t m", t=PACK))
+
+        b_ps = [ps.tile([P, J], F32, name="b_ps%d" % t) for t in range(PACK)]
+        for t in range(PACK):
+            cols = slice(P * t, P * (t + 1))
+            nc.tensor.matmul_mx(b_ps[t][:], lhsT=w_pw[:, cols].bitcast(E5M2), lhsT_scale=w_ps[:, cols],
+                                rhs=xo_gw[:].bitcast(E2M1), rhs_scale=xo_gs[:], start=True, stop=True)
+
+        xt_gw = sbuf("xt_gw", J, U32)
+        xt_gs = sbuf("xt_gs", J, U8)
+        nc.vector.tensor_copy(xt_gw[:], xt_w[:].indirect(l1[:]))
+        nc.vector.tensor_copy(xt_gs[:], xt_s[:].indirect(l1[:]))
+        a_ps = [ps.tile([P, 2 * J], F32, name="a_ps%d" % u) for u in range(2)]
+        for t in range(PACK):
+            cols = slice(P * t, P * (t + 1))
+            nc.tensor.matmul_mx(a_ps[t // 2][:, J * (t % 2) : J * (t % 2 + 1)], lhsT=w_pw[:, cols].bitcast(E5M2), lhsT_scale=w_ps[:, cols],
+                                rhs=xt_gw[:].bitcast(E4M3), rhs_scale=xt_gs[:], start=True, stop=True)
+
+        for t in range(PACK):
+            nc.scalar.copy(b_sb[t][:, :J], b_ps[t][:])
+            nc.scalar.activation(h_sb[t][:, J:], b_sb[t][:].indirect(l3[:]), ACT.Copy)
+
+        diff = sb.tile([P, PACK, J], F32, name="diff", align_bytes=64)
+        kept = sb.tile([P, 2, J], F32, name="kept", align_bytes=64)
+        for t in range(PACK):
+            nc.vector.tensor_tensor(h_sb[t][:, :J], a_ps[t // 2][:, J * (t % 2) : J * (t % 2 + 1)], h_sb[t][:, J:], ALU.max)
+            if t < 2:
+                nc.vector.tensor_tensor(diff[:, t, :], h_sb[t][:].indirect(l4[:]), b_sb[t][:, :J], ALU.subtract)
+            else:
+                nc.scalar.activation(kept[:, t - 2, :], h_sb[t][:].indirect(l4[:]), ACT.Copy)
+
+        vs_gw = sbuf("vs_gw", N, U32)
+        vs_gs = sbuf("vs_gs", N, U8)
+        nc.vector.tensor_copy(vs_gw[:], vs_w[:].indirect(l5[:]))
+        nc.vector.tensor_copy(vs_gs[:], vs_s[:].indirect(l5[:]))
+        for t in range(2, PACK):
+            nc.vector.tensor_tensor(diff[:, t, :], kept[:, t - 2, :], b_sb[t][:, :J], ALU.subtract)
+
+        hid = sb.tile([P, J, PACK], BF16, name="hid", align_bytes=64)
+        woven = diff[:].rearrange("p t j -> p j t")
+        half = J // 2
+        nc.scalar.activation(hid[:, :half, :], woven[:, :half, :], ACT.Abs)
+        nc.vector.scalar_tensor_tensor(hid[:, half:, :], woven[:, half:, :], -1.0, woven[:, half:, :], ALU.mult, ALU.max)
+
+        hid_w = sbuf("hid_w", J, U32)
+        hid_s = sbuf("hid_s", J, U8)
+        nc.vector.quantize_mx(out=hid_w[:].bitcast(E4M3), scales=hid_s[:], in_=hid[:].rearrange("p j t -> p (j t)"))
+
+        for u in range(2):
+            cols = slice(P * u, P * (u + 1))
+            y_ps = ps.tile([P, J], F32, name="y_ps%d" % u)
+            nc.tensor.matmul_mx(y_ps[:], lhsT=vs_gw[:, cols].bitcast(E5M2), lhsT_scale=vs_gs[:, cols],
+                                rhs=hid_w[:].bitcast(E4M3), rhs_scale=hid_s[:], start=True, stop=True)
+            y_sb = sbuf("y_sb%d" % u, J, F32)
+            if u == 0:
+                nc.scalar.copy(y_sb[:], y_ps[:])
+                nc.scalar.dma_start(out[cols, :], y_sb[:])
+            else:
+                nc.vector.tensor_copy(y_sb[:], y_ps[:])
+                nc.sync.dma_start(out[cols, :], y_sb[:])

@@ -18,7 +18,7 @@ ALU = mybir.AluOpType
 ACT = mybir.ActivationFunctionType
 P = 128
 PACK = 4
-B_WINDOW = 352
+B_WINDOW = 264
 
 
 def tile_list_tworounds_oneforboth_store_plain_kernel(tc, xt_words, xt_scales, xo_words, xo_scales, w_words, w_scales, vs_words, vs_scales,
@@ -57,39 +57,41 @@ def tile_list_tworounds_oneforboth_store_plain_kernel(tc, xt_words, xt_scales, x
         nc.gpsimd.memset(w_s[:].bitcast(I32), 0)
         nc.vector.memset(xt_s[:].bitcast(I32), 0)
         nc.vector.memset(vs_s[:].bitcast(I32), 0)
+        for t in range(PACK):
+            nc.vector.memset(b_sb[t][:, J:], 0.0)
 
         l2 = load_list("l2", offs2)
-        load_words(nc.sync, xo_w, xo_words[0])
         load_words(nc.sync, w_w, w_words[0].rearrange("p n t -> p (n t)"))
         for q in range(4):
-            load_scale_rows(nc.scalar, xo_s, xo_scales, q)
-        load_scale_rows(nc.scalar, w_s, w_scales, 0)
-        load_scale_rows(nc.gpsimd, w_s, w_scales, 2)
-        load_scale_rows(nc.gpsimd, w_s, w_scales, 3)
-        load_scale_rows(nc.sync, w_s, w_scales, 1)
-        l1 = load_list("l1", offs)
+            load_scale_rows(nc.sync, xo_s, xo_scales, q)
+        load_words(nc.sync, xo_w, xo_words[0])
         load_words(nc.sync, xt_w, xt_words[0].rearrange("p n t -> p (n t)"))
+        load_scale_rows(nc.gpsimd, w_s, w_scales, 3)
+        for q in range(3):
+            load_scale_rows(nc.sync, w_s, w_scales, q)
+        l1 = load_list("l1", offs)
         for q in range(4):
             load_scale_rows(nc.sync, xt_s, xt_scales, q)
         l3 = load_list("l3", offs3)
+        load_words(nc.sync, vs_w, vs_words[0].rearrange("p n t -> p (n t)"))
         l4 = load_list("l4", offs4)
         l5 = load_list("l5", offs5)
-        load_words(nc.sync, vs_w, vs_words[0].rearrange("p n t -> p (n t)"))
         for q in range(4):
-            load_scale_rows(nc.sync, vs_s, vs_scales, q)
-        for t in range(PACK):
-            nc.gpsimd.memset(b_sb[t][:, J:], 0.0)
+            load_scale_rows(nc.gpsimd, vs_s, vs_scales, q)
 
         xo_gw = sbuf("xo_gw", J, U16)
         xo_gs = sbuf("xo_gs", J, U8)
-        nc.vector.tensor_copy(xo_gw[:], xo_w[:].indirect(l2[:]))
-        nc.vector.tensor_copy(xo_gs[:], xo_s[:].indirect(l2[:]))
         w_pw = sbuf("w_pw", R, U32)
         w_ps = sbuf("w_ps", R, U8)
         nc.vector.tensor_copy(w_pw[:].rearrange("p (t m) -> p t m", t=PACK), w_w[:].rearrange("p (m t) -> p t m", t=PACK))
-        nc.vector.tensor_copy(w_ps[:].rearrange("p (t m) -> p t m", t=PACK), w_s[:].rearrange("p (m t) -> p t m", t=PACK))
+        nc.vector.tensor_copy(xo_gw[:], xo_w[:].indirect(l2[:]))
+        nc.vector.tensor_copy(xo_gs[:], xo_s[:].indirect(l2[:]))
+        dealt_out = w_ps[:].rearrange("p (t m) -> p t m", t=PACK)
+        dealt_in = w_s[:].rearrange("p (m t) -> p t m", t=PACK)
+        nc.vector.tensor_copy(dealt_out[:, :2, :], dealt_in[:, :2, :])
+        nc.vector.tensor_copy(dealt_out[:, 2:, :], dealt_in[:, 2:, :])
 
-        b_ps = [ps.tile([P, J], F32, name="b_ps%d" % t) for t in range(PACK)]
+        b_ps = [ps.tile([P, J], F32, name="b_ps%d" % t, tag="bank%d" % t) for t in range(PACK)]
         for t in range(PACK):
             cols = slice(P * t, P * (t + 1))
             nc.tensor.matmul_mx(b_ps[t][:], lhsT=w_pw[:, cols].bitcast(E5M2), lhsT_scale=w_ps[:, cols],
@@ -99,45 +101,44 @@ def tile_list_tworounds_oneforboth_store_plain_kernel(tc, xt_words, xt_scales, x
         xt_gs = sbuf("xt_gs", J, U8)
         nc.vector.tensor_copy(xt_gw[:], xt_w[:].indirect(l1[:]))
         nc.vector.tensor_copy(xt_gs[:], xt_s[:].indirect(l1[:]))
-        a_ps = [ps.tile([P, 2 * J], F32, name="a_ps%d" % u) for u in range(2)]
+        a_ps = [ps.tile([P, J], F32, name="a_ps%d" % t) for t in range(PACK)]
         for t in range(PACK):
             cols = slice(P * t, P * (t + 1))
-            nc.tensor.matmul_mx(a_ps[t // 2][:, J * (t % 2) : J * (t % 2 + 1)], lhsT=w_pw[:, cols].bitcast(E5M2), lhsT_scale=w_ps[:, cols],
+            nc.tensor.matmul_mx(a_ps[t][:], lhsT=w_pw[:, cols].bitcast(E5M2), lhsT_scale=w_ps[:, cols],
                                 rhs=xt_gw[:].bitcast(E4M3), rhs_scale=xt_gs[:], start=True, stop=True)
 
         for t in range(PACK):
             nc.scalar.copy(b_sb[t][:, :J], b_ps[t][:])
             nc.scalar.activation(h_sb[t][:, J:], b_sb[t][:].indirect(l3[:]), ACT.Copy)
 
-        diff = sb.tile([P, PACK, J], F32, name="diff", align_bytes=64)
-        kept = sb.tile([P, 2, J], F32, name="kept", align_bytes=64)
-        for t in range(PACK):
-            nc.vector.tensor_tensor(h_sb[t][:, :J], a_ps[t // 2][:, J * (t % 2) : J * (t % 2 + 1)], h_sb[t][:, J:], ALU.max)
-            if t < 2:
-                nc.vector.tensor_tensor(diff[:, t, :], h_sb[t][:].indirect(l4[:]), b_sb[t][:, :J], ALU.subtract)
-            else:
-                nc.scalar.activation(kept[:, t - 2, :], h_sb[t][:].indirect(l4[:]), ACT.Copy)
-
         vs_gw = sbuf("vs_gw", N, U32)
         vs_gs = sbuf("vs_gs", N, U8)
-        nc.vector.tensor_copy(vs_gw[:], vs_w[:].indirect(l5[:]))
-        nc.vector.tensor_copy(vs_gs[:], vs_s[:].indirect(l5[:]))
-        for t in range(2, PACK):
-            nc.vector.tensor_tensor(diff[:, t, :], kept[:, t - 2, :], b_sb[t][:, :J], ALU.subtract)
+        diff = sb.tile([P, PACK, J], F32, name="diff", align_bytes=64)
+        kept = sb.tile([P, PACK - 1, J], F32, name="kept", align_bytes=64)
+        for t in range(PACK):
+            nc.vector.tensor_tensor(h_sb[t][:, :J], a_ps[t][:], h_sb[t][:, J:], ALU.max)
+            if t == PACK - 1:
+                nc.vector.tensor_tensor(diff[:, t, :], h_sb[t][:].indirect(l4[:]), b_sb[t][:, :J], ALU.subtract)
+            else:
+                nc.scalar.activation(kept[:, t, :], h_sb[t][:].indirect(l4[:]), ACT.Copy)
+            if t == 1:
+                nc.vector.tensor_copy(vs_gw[:], vs_w[:].indirect(l5[:]))
+        for t in range(PACK - 1):
+            nc.vector.tensor_tensor(diff[:, t, :], kept[:, t, :], b_sb[t][:, :J], ALU.subtract)
 
         hid = sb.tile([P, J, PACK], BF16, name="hid", align_bytes=64)
         woven = diff[:].rearrange("p t j -> p j t")
-        half = J // 2
-        nc.scalar.activation(hid[:, :half, :], woven[:, :half, :], ACT.Abs)
-        nc.vector.scalar_tensor_tensor(hid[:, half:, :], woven[:, half:, :], -1.0, woven[:, half:, :], ALU.mult, ALU.max)
+        share = 176
+        nc.scalar.activation(hid[:, :share, :], woven[:, :share, :], ACT.Abs)
+        nc.vector.scalar_tensor_tensor(hid[:, share:, :], woven[:, share:, :], -1.0, woven[:, share:, :], ALU.mult, ALU.max)
+        nc.vector.tensor_copy(vs_gs[:], vs_s[:].indirect(l5[:]))
 
         hid_w = sbuf("hid_w", J, U32)
         hid_s = sbuf("hid_s", J, U8)
         nc.vector.quantize_mx(out=hid_w[:].bitcast(E4M3), scales=hid_s[:], in_=hid[:].rearrange("p j t -> p (j t)"))
-
         for u in range(2):
             cols = slice(P * u, P * (u + 1))
-            y_ps = ps.tile([P, J], F32, name="y_ps%d" % u)
+            y_ps = ps.tile([P, J], F32, name="y_ps%d" % u, tag="bank%d" % u)
             nc.tensor.matmul_mx(y_ps[:], lhsT=vs_gw[:, cols].bitcast(E5M2), lhsT_scale=vs_gs[:, cols],
                                 rhs=hid_w[:].bitcast(E4M3), rhs_scale=hid_s[:], start=True, stop=True)
             y_sb = sbuf("y_sb%d" % u, J, F32)

@@ -19,6 +19,7 @@ ACT = mybir.ActivationFunctionType
 P = 128
 PACK = 4
 B_WINDOW = 264
+B_WINDOW_V = 352
 
 
 def tile_list_tworounds_oneforboth_store_plain_kernel(tc, xt_words, xt_scales, xo_words, xo_scales, w_words, w_scales, vs_words, vs_scales,
@@ -47,11 +48,10 @@ def tile_list_tworounds_oneforboth_store_plain_kernel(tc, xt_words, xt_scales, x
         w_w = sbuf("w_w", R, U32)
         w_s = sbuf("w_s", R, U8)
         xt_w = sbuf("xt_w", T, U32)
-        xt_s = sbuf("xt_s", T, U8)
+        xt_s = sb.tile([P, T], U8, name="xt_s", tag="h_sb1", align_bytes=64)
         vs_w = sbuf("vs_w", T, U32)
         vs_s = sbuf("vs_s", T, U8)
-        b_sb = [sbuf("b_sb%d" % t, B_WINDOW, F32) for t in range(PACK)]
-        h_sb = [sbuf("h_sb%d" % t, 2 * J, F32) for t in range(PACK)]
+        b_sb = [sbuf("b_sb%d" % t, B_WINDOW_V if t == 1 else B_WINDOW, F32) for t in range(PACK)]
 
         nc.vector.memset(xo_s[:].bitcast(I32), 0)
         nc.gpsimd.memset(w_s[:].bitcast(I32), 0)
@@ -70,9 +70,9 @@ def tile_list_tworounds_oneforboth_store_plain_kernel(tc, xt_words, xt_scales, x
         for q in range(3):
             load_scale_rows(nc.sync, w_s, w_scales, q)
         l1 = load_list("l1", offs)
+        l3 = load_list("l3", offs3)
         for q in range(4):
             load_scale_rows(nc.sync, xt_s, xt_scales, q)
-        l3 = load_list("l3", offs3)
         load_words(nc.sync, vs_w, vs_words[0].rearrange("p n t -> p (n t)"))
         l4 = load_list("l4", offs4)
         l5 = load_list("l5", offs5)
@@ -100,6 +100,8 @@ def tile_list_tworounds_oneforboth_store_plain_kernel(tc, xt_words, xt_scales, x
         xt_gw = sbuf("xt_gw", J, U32)
         xt_gs = sbuf("xt_gs", J, U8)
         nc.vector.tensor_copy(xt_gw[:], xt_w[:].indirect(l1[:]))
+        for t in (1, 2):
+            nc.vector.tensor_copy(b_sb[t][:, :J], b_ps[t][:])
         nc.vector.tensor_copy(xt_gs[:], xt_s[:].indirect(l1[:]))
         a_ps = [ps.tile([P, J], F32, name="a_ps%d" % t) for t in range(PACK)]
         for t in range(PACK):
@@ -107,44 +109,50 @@ def tile_list_tworounds_oneforboth_store_plain_kernel(tc, xt_words, xt_scales, x
             nc.tensor.matmul_mx(a_ps[t][:], lhsT=w_pw[:, cols].bitcast(E5M2), lhsT_scale=w_ps[:, cols],
                                 rhs=xt_gw[:].bitcast(E4M3), rhs_scale=xt_gs[:], start=True, stop=True)
 
-        for t in range(PACK):
-            nc.scalar.copy(b_sb[t][:, :J], b_ps[t][:])
+        h_sb = [sb.tile([P, 2 * J], F32, name="h_sb%d" % t, tag="h_sb%d" % t, align_bytes=64) for t in range(PACK)]
+        nc.scalar.copy(b_sb[0][:, :J], b_ps[0][:])
+        nc.scalar.activation(h_sb[0][:, J:], b_sb[0][:].indirect(l3[:]), ACT.Copy)
+        nc.scalar.copy(b_sb[3][:, :J], b_ps[3][:])
+        nc.vector.tensor_copy(h_sb[1][:, J:], b_sb[1][:].indirect(l3[:]))
+        for t in (2, 3):
             nc.scalar.activation(h_sb[t][:, J:], b_sb[t][:].indirect(l3[:]), ACT.Copy)
 
-        vs_gw = sbuf("vs_gw", N, U32)
-        vs_gs = sbuf("vs_gs", N, U8)
         diff = sb.tile([P, PACK, J], F32, name="diff", align_bytes=64)
-        kept = sb.tile([P, PACK - 1, J], F32, name="kept", align_bytes=64)
+        kept = [sb.tile([P, J], F32, name="kept%d" % t, tag="kept%d" % t, align_bytes=64) for t in range(PACK - 1)]
         for t in range(PACK):
             nc.vector.tensor_tensor(h_sb[t][:, :J], a_ps[t][:], h_sb[t][:, J:], ALU.max)
-            if t == PACK - 1:
-                nc.vector.tensor_tensor(diff[:, t, :], h_sb[t][:].indirect(l4[:]), b_sb[t][:, :J], ALU.subtract)
-            else:
-                nc.scalar.activation(kept[:, t, :], h_sb[t][:].indirect(l4[:]), ACT.Copy)
-            if t == 1:
-                nc.vector.tensor_copy(vs_gw[:], vs_w[:].indirect(l5[:]))
         for t in range(PACK - 1):
-            nc.vector.tensor_tensor(diff[:, t, :], kept[:, t, :], b_sb[t][:, :J], ALU.subtract)
+            nc.scalar.activation(kept[t][:], h_sb[t][:].indirect(l4[:]), ACT.Copy)
+        nc.vector.tensor_tensor(diff[:, 3, :], h_sb[3][:].indirect(l4[:]), b_sb[3][:, :J], ALU.subtract)
+        for t in range(PACK - 1):
+            nc.vector.tensor_tensor(diff[:, t, :], kept[t][:], b_sb[t][:, :J], ALU.subtract)
 
         hid = sb.tile([P, J, PACK], BF16, name="hid", align_bytes=64)
-        woven = diff[:].rearrange("p t j -> p j t")
-        share = 176
-        nc.scalar.activation(hid[:, :share, :], woven[:, :share, :], ACT.Abs)
-        nc.vector.scalar_tensor_tensor(hid[:, share:, :], woven[:, share:, :], -1.0, woven[:, share:, :], ALU.mult, ALU.max)
+        half = J // 2
+        for v in range(2):
+            slots = slice(half * v, half * (v + 1))
+            nc.scalar.activation(hid[:, slots, :].rearrange("p (c i) t -> p c t i", i=4), diff[:, :, slots].rearrange("p t (c i) -> p c t i", i=4), ACT.Abs)
+        vs_gw = sb.tile([P, N], U32, name="vs_gw", tag="kept0", align_bytes=64)
+        vs_gs = sb.tile([P, N], U8, name="vs_gs", tag="kept2", align_bytes=64)
+        nc.vector.tensor_copy(vs_gw[:], vs_w[:].indirect(l5[:]))
         nc.vector.tensor_copy(vs_gs[:], vs_s[:].indirect(l5[:]))
 
         hid_w = sbuf("hid_w", J, U32)
         hid_s = sbuf("hid_s", J, U8)
-        nc.vector.quantize_mx(out=hid_w[:].bitcast(E4M3), scales=hid_s[:], in_=hid[:].rearrange("p j t -> p (j t)"))
-        for u in range(2):
-            cols = slice(P * u, P * (u + 1))
-            y_ps = ps.tile([P, J], F32, name="y_ps%d" % u, tag="bank%d" % u)
-            nc.tensor.matmul_mx(y_ps[:], lhsT=vs_gw[:, cols].bitcast(E5M2), lhsT_scale=vs_gs[:, cols],
-                                rhs=hid_w[:].bitcast(E4M3), rhs_scale=hid_s[:], start=True, stop=True)
-            y_sb = sbuf("y_sb%d" % u, J, F32)
-            if u == 0:
-                nc.scalar.copy(y_sb[:], y_ps[:])
-                nc.scalar.dma_start(out[cols, :], y_sb[:])
-            else:
-                nc.vector.tensor_copy(y_sb[:], y_ps[:])
-                nc.sync.dma_start(out[cols, :], y_sb[:])
+        for v in range(2):
+            slots = slice(half * v, half * (v + 1))
+            nc.vector.quantize_mx(out=hid_w[:, slots].bitcast(E4M3), scales=hid_s[:, slots], in_=hid[:, slots, :].rearrange("p j t -> p (j t)"))
+        for v in range(2):
+            slots = slice(half * v, half * (v + 1))
+            for u in range(2):
+                cols = slice(P * u, P * (u + 1))
+                y_ps = ps.tile([P, half], F32, name="y_ps%d%d" % (u, v), tag="bank%d" % (2 * v + u))
+                nc.tensor.matmul_mx(y_ps[:], lhsT=vs_gw[:, cols].bitcast(E5M2), lhsT_scale=vs_gs[:, cols],
+                                    rhs=hid_w[:, slots].bitcast(E4M3), rhs_scale=hid_s[:, slots], start=True, stop=True)
+                y_sb = sbuf("y_sb%d%d" % (u, v), half, F32)
+                if u == 0:
+                    nc.scalar.copy(y_sb[:], y_ps[:])
+                    nc.scalar.dma_start(out[cols, slots], y_sb[:])
+                else:
+                    nc.vector.tensor_copy(y_sb[:], y_ps[:])
+                    nc.sync.dma_start(out[cols, slots], y_sb[:])

@@ -73,9 +73,9 @@ def tile_list_tworounds_oneforboth_store_plain_kernel(tc, xt_words, xt_scales, x
         l3 = load_list("l3", offs3)
         for q in range(4):
             load_scale_rows(nc.sync, xt_s, xt_scales, q)
-        load_words(nc.sync, vs_w, vs_words[0].rearrange("p n t -> p (n t)"))
         l4 = load_list("l4", offs4)
         l5 = load_list("l5", offs5)
+        load_words(nc.sync, vs_w, vs_words[0].rearrange("p n t -> p (n t)"))
         for q in range(4):
             load_scale_rows(nc.gpsimd, vs_s, vs_scales, q)
 

from contextlib import ExitStack

import concourse.mybir as mybir

K, T, J, R, N = 512, 1024, 256, 512, 256
FLOPS = 2 * (2 * K * R * J + R * N * J)

F32 = mybir.dt.float32
BF16 = mybir.dt.bfloat16
I32 = mybir.dt.int32
U32 = mybir.dt.uint32
U16 = mybir.dt.uint16
U8 = mybir.dt.uint8
E4M3 = mybir.dt.float8_e4m3fn_x4
E5M2 = mybir.dt.float8_e5m2_x4
E2M1 = mybir.dt.float4_e2m1fn_x4
ALU = mybir.AluOpType
ACT = mybir.ActivationFunctionType
P = 128
PACK = 4
B_WINDOW = 264
B_WINDOW_V = 352


def tile_list_tworounds_oneforboth_store_plain_kernel(tc, xt_words, xt_scales, xo_words, xo_scales, w_words, w_scales, vs_words, vs_scales,
                        offs, offs2, offs3, offs4, offs5, out):
    nc = tc.nc
    with ExitStack() as ctx:
        sb = ctx.enter_context(tc.tile_pool(name="sb", bufs=1))
        ps = ctx.enter_context(tc.psum_pool(name="ps", bufs=1))

        def sbuf(name, cols, dtype):
            return sb.tile([P, cols], dtype, name=name, align_bytes=64)

        def load_list(name, src):
            lst = sb.tile([P, J // 16], U16, name=name)
            nc.sync.dma_start(lst[:], src)
            return lst

        def load_words(queue, tile, src):
            queue.dma_start(tile[:].bitcast(I32), src.bitcast(I32))

        def load_scale_rows(queue, plane, src, q):
            queue.dma_start(plane[32 * q : 32 * q + 4, :].bitcast(I32), src[0, 4 * q : 4 * q + 4, :].bitcast(I32))

        xo_w = sbuf("xo_w", T, U16)
        xo_s = sbuf("xo_s", T, U8)
        w_w = sbuf("w_w", R, U32)
        w_s = sbuf("w_s", R, U8)
        xt_w = sbuf("xt_w", T, U32)
        xt_s = sb.tile([P, T], U8, name="xt_s", tag="h_sb1", align_bytes=64)
        vs_w = sbuf("vs_w", T, U32)
        vs_s = sbuf("vs_s", T, U8)
        b_sb = [sbuf("b_sb%d" % t, B_WINDOW_V if t == 1 else B_WINDOW, F32) for t in range(PACK)]

        nc.vector.memset(xo_s[:].bitcast(I32), 0)
        nc.gpsimd.memset(w_s[:].bitcast(I32), 0)
        nc.vector.memset(xt_s[:].bitcast(I32), 0)
        nc.vector.memset(vs_s[:].bitcast(I32), 0)
        for t in range(PACK):
            nc.vector.memset(b_sb[t][:, J:], 0.0)

        l2 = load_list("l2", offs2)
        load_words(nc.sync, w_w, w_words[0].rearrange("p n t -> p (n t)"))
        for q in range(4):
            load_scale_rows(nc.sync, xo_s, xo_scales, q)
        load_words(nc.sync, xo_w, xo_words[0])
        load_words(nc.sync, xt_w, xt_words[0].rearrange("p n t -> p (n t)"))
        load_scale_rows(nc.gpsimd, w_s, w_scales, 3)
        for q in range(3):
            load_scale_rows(nc.sync, w_s, w_scales, q)
        l1 = load_list("l1", offs)
        l3 = load_list("l3", offs3)
        for q in range(4):
            load_scale_rows(nc.sync, xt_s, xt_scales, q)
        l4 = load_list("l4", offs4)
        l5 = load_list("l5", offs5)
        load_words(nc.sync, vs_w, vs_words[0].rearrange("p n t -> p (n t)"))
        for q in range(4):
            load_scale_rows(nc.gpsimd, vs_s, vs_scales, q)

        xo_gw = sbuf("xo_gw", J, U16)
        xo_gs = sbuf("xo_gs", J, U8)
        w_pw = sbuf("w_pw", R, U32)
        w_ps = sbuf("w_ps", R, U8)
        nc.vector.tensor_copy(w_pw[:].rearrange("p (t m) -> p t m", t=PACK), w_w[:].rearrange("p (m t) -> p t m", t=PACK))
        nc.vector.tensor_copy(xo_gw[:], xo_w[:].indirect(l2[:]))
        nc.vector.tensor_copy(xo_gs[:], xo_s[:].indirect(l2[:]))
        dealt_out = w_ps[:].rearrange("p (t m) -> p t m", t=PACK)
        dealt_in = w_s[:].rearrange("p (m t) -> p t m", t=PACK)
        nc.vector.tensor_copy(dealt_out[:, :2, :], dealt_in[:, :2, :])
        nc.vector.tensor_copy(dealt_out[:, 2:, :], dealt_in[:, 2:, :])

        b_ps = [ps.tile([P, J], F32, name="b_ps%d" % t, tag="bank%d" % t) for t in range(PACK)]
        for t in range(PACK):
            cols = slice(P * t, P * (t + 1))
            nc.tensor.matmul_mx(b_ps[t][:], lhsT=w_pw[:, cols].bitcast(E5M2), lhsT_scale=w_ps[:, cols],
                                rhs=xo_gw[:].bitcast(E2M1), rhs_scale=xo_gs[:], start=True, stop=True)

        xt_gw = sbuf("xt_gw", J, U32)
        xt_gs = sbuf("xt_gs", J, U8)
        nc.vector.tensor_copy(xt_gw[:], xt_w[:].indirect(l1[:]))
        for t in (1, 2):
            nc.vector.tensor_copy(b_sb[t][:, :J], b_ps[t][:])
        nc.vector.tensor_copy(xt_gs[:], xt_s[:].indirect(l1[:]))
        a_ps = [ps.tile([P, J], F32, name="a_ps%d" % t) for t in range(PACK)]
        for t in range(PACK):
            cols = slice(P * t, P * (t + 1))
            nc.tensor.matmul_mx(a_ps[t][:], lhsT=w_pw[:, cols].bitcast(E5M2), lhsT_scale=w_ps[:, cols],
                                rhs=xt_gw[:].bitcast(E4M3), rhs_scale=xt_gs[:], start=True, stop=True)

        h_sb = [sb.tile([P, 2 * J], F32, name="h_sb%d" % t, tag="h_sb%d" % t, align_bytes=64) for t in range(PACK)]
        nc.scalar.copy(b_sb[0][:, :J], b_ps[0][:])
        nc.scalar.activation(h_sb[0][:, J:], b_sb[0][:].indirect(l3[:]), ACT.Copy)
        nc.scalar.copy(b_sb[3][:, :J], b_ps[3][:])
        nc.vector.tensor_copy(h_sb[1][:, J:], b_sb[1][:].indirect(l3[:]))
        for t in (2, 3):
            nc.scalar.activation(h_sb[t][:, J:], b_sb[t][:].indirect(l3[:]), ACT.Copy)

        diff = sb.tile([P, PACK, J], F32, name="diff", align_bytes=64)
        kept = [sb.tile([P, J], F32, name="kept%d" % t, tag="kept%d" % t, align_bytes=64) for t in range(PACK - 1)]
        for t in range(PACK):
            nc.vector.tensor_tensor(h_sb[t][:, :J], a_ps[t][:], h_sb[t][:, J:], ALU.max)
        for t in range(PACK - 1):
            nc.scalar.activation(kept[t][:], h_sb[t][:].indirect(l4[:]), ACT.Copy)
        nc.vector.tensor_tensor(diff[:, 3, :], h_sb[3][:].indirect(l4[:]), b_sb[3][:, :J], ALU.subtract)
        for t in range(PACK - 1):
            nc.vector.tensor_tensor(diff[:, t, :], kept[t][:], b_sb[t][:, :J], ALU.subtract)

        hid = sb.tile([P, J, PACK], BF16, name="hid", align_bytes=64)
        half = J // 2
        for v in range(2):
            slots = slice(half * v, half * (v + 1))
            nc.scalar.activation(hid[:, slots, :].rearrange("p (c i) t -> p c t i", i=4), diff[:, :, slots].rearrange("p t (c i) -> p c t i", i=4), ACT.Abs)
        vs_gw = sb.tile([P, N], U32, name="vs_gw", tag="kept0", align_bytes=64)
        vs_gs = sb.tile([P, N], U8, name="vs_gs", tag="kept2", align_bytes=64)
        nc.vector.tensor_copy(vs_gw[:], vs_w[:].indirect(l5[:]))
        nc.vector.tensor_copy(vs_gs[:], vs_s[:].indirect(l5[:]))

        hid_w = sbuf("hid_w", J, U32)
        hid_s = sbuf("hid_s", J, U8)
        for v in range(2):
            slots = slice(half * v, half * (v + 1))
            nc.vector.quantize_mx(out=hid_w[:, slots].bitcast(E4M3), scales=hid_s[:, slots], in_=hid[:, slots, :].rearrange("p j t -> p (j t)"))
        for v in range(2):
            slots = slice(half * v, half * (v + 1))
            for u in range(2):
                cols = slice(P * u, P * (u + 1))
                y_ps = ps.tile([P, half], F32, name="y_ps%d%d" % (u, v), tag="bank%d" % (2 * v + u))
                nc.tensor.matmul_mx(y_ps[:], lhsT=vs_gw[:, cols].bitcast(E5M2), lhsT_scale=vs_gs[:, cols],
                                    rhs=hid_w[:, slots].bitcast(E4M3), rhs_scale=hid_s[:, slots], start=True, stop=True)
                y_sb = sbuf("y_sb%d%d" % (u, v), half, F32)
                if u == 0:
                    nc.scalar.copy(y_sb[:], y_ps[:])
                    nc.scalar.dma_start(out[cols, slots], y_sb[:])
                else:
                    nc.vector.tensor_copy(y_sb[:], y_ps[:])
                    nc.sync.dma_start(out[cols, slots], y_sb[:])
